import numpy as np
import ml_dtypes


def mxq(x, axis, fmt="e4m3"):
    dtype, down = {"e4m3": (ml_dtypes.float8_e4m3fn, 7), "e5m2": (ml_dtypes.float8_e5m2, 14)}[fmt]
    v = np.moveaxis(np.asarray(x, np.float32).astype(ml_dtypes.bfloat16).astype(np.float64), axis, -1)
    blocks = v.reshape(v.shape[:-1] + (-1, 32))
    amax = np.abs(blocks).max(-1, keepdims=True)
    byte = np.maximum(np.where(amax > 0, np.frexp(amax)[1] - 1 + 127, 0) - down, 1)
    scale = np.exp2(byte - 127.0)
    codes = (blocks / scale).astype(np.float32).astype(dtype).astype(np.float64)
    return np.moveaxis((codes * scale).reshape(v.shape), -1, axis)


WIDE = False


def mx_kscale(k):
    if not WIDE:
        return np.ones(k)
    levels = np.array([10, -10, 5, -5, 0])
    if k % 512:
        return np.exp2(np.random.permutation(np.resize(levels, k // 32))).repeat(32)
    a = np.empty((k // 512, 16))
    for p in range(k // 512):
        a[p, :8] = np.random.permutation(np.resize(levels, 8))
        for g in range(8):
            far = levels[np.abs(levels - a[p, g]) >= 10]
            a[p, g + 8] = far[np.random.randint(len(far))]
    return np.exp2(a.ravel()).repeat(32)


BF16 = ml_dtypes.bfloat16


def bf(x):
    return np.asarray(x, np.float32).astype(BF16)


def f64(x):
    return np.asarray(x).astype(np.float64)


E2M1 = np.array([0.0, 0.5, 1.0, 1.5, 2.0, 3.0, 4.0, 6.0, -0.0, -0.5, -1.0, -1.5, -2.0, -3.0, -4.0, -6.0])


def pack_weight(w, fmt):
    k, n = w.shape
    w = f64(bf(w)).reshape(k // 32, 32, n)
    amax = np.abs(w).max(1)
    if fmt == "e4m3":
        byte = np.frexp(amax)[1] - 1 + 127 - 7
    else:
        mant, ex = np.frexp(amax / 6.0)
        byte = np.where(mant > 0.5, ex, ex - 1) + 127
    byte = np.clip(np.where(amax > 0, byte, 1), 1, 254)
    scaled = (w * np.exp2(127.0 - byte)[:, None, :]).reshape(k, n).astype(np.float32)
    by_word = np.ascontiguousarray(scaled.reshape(k // 512, 128, 4, n).transpose(0, 1, 3, 2))
    if fmt == "e4m3":
        words = by_word.astype(ml_dtypes.float8_e4m3fn).view(np.uint8)
    else:
        c = by_word.astype(ml_dtypes.float4_e2m1fn).view(np.uint8) & 0xF
        words = c[..., 0::2] | (c[..., 1::2] << 4)
    return np.ascontiguousarray(words), np.ascontiguousarray(byte.astype(np.uint8).reshape(k // 512, 16, n))


def unpack_weight(words, scales, fmt):
    g, p, n, _ = words.shape
    if fmt == "e4m3":
        vals = np.ascontiguousarray(words).view(ml_dtypes.float8_e4m3fn).astype(np.float64)
    else:
        nib = np.empty((g, p, n, 4), np.uint8)
        nib[..., 0::2] = words & 0xF
        nib[..., 1::2] = words >> 4
        vals = E2M1[nib]
    vals = vals * np.repeat(np.exp2(scales.astype(np.float64) - 127.0), 8, axis=1)[..., None]
    return vals.transpose(0, 1, 3, 2).reshape(g * 512, n)
def pack4(w):
    words, scales = pack_weight(w, "e2m1")
    return words.reshape(words.shape[0], 128, -1), scales


def unpack4(words, scales):
    return unpack_weight(words.reshape(words.shape[0], 128, -1, 2), scales, "e2m1")


def planes(Y):
    n, m = Y.shape
    b = f64(bf(Y)).reshape(n // 32, 32, m)
    amax = np.abs(b).max(1)
    byte = np.clip(np.where(amax > 0, np.frexp(amax)[1] - 1 + 127 - 7, 1), 1, 254)
    codes = (b * np.exp2(127.0 - byte)[:, None, :]).reshape(n, m).astype(np.float32).astype(ml_dtypes.float8_e4m3fn).view(np.uint8)
    words = codes.reshape(n // 512, 128, 4, m).transpose(0, 1, 3, 2)
    return np.ascontiguousarray(words), np.ascontiguousarray(byte.astype(np.uint8).reshape(n // 512, 16, m))


F, N, D, P = 2, 1024, 1024, 512

def setup_inputs():
    s = mx_kscale(N)[None, :, None]
    u = mx_kscale(F * N).reshape(F, N)
    T = np.random.randn(F, N, D)
    O = np.random.randn(F, N, P)
    h = np.random.randn(F, N, N) / np.sqrt(N) * s
    h_words, h_scales = pack_weight(h.reshape(F * N, N), "e4m3")
    t_words, t_scales = pack4((T[::-1] / s).reshape(F * N, D))
    return {
        "h_words": h_words, "h_scales": h_scales,
        "t_words": t_words, "t_scales": t_scales,
        "o_train": bf(O[::-1] / s),
        "t_own": bf(T), "o_own": bf(O),
        "a": bf(np.exp(0.3 * np.random.randn(F, N)) * u),
        "b": bf(np.exp(0.3 * np.random.randn(F, N)) / u),
        "earlier": bf(np.sqrt(F * N) * np.random.randn(D, P)),
        "gain": bf(np.exp(0.8 * np.random.randn(D)) / (2 * np.sqrt(F * N))),
    }

def reference(h_words, h_scales, t_words, t_scales, o_train, t_own, o_own, a, b, earlier, gain):
    H = unpack_weight(h_words, h_scales, "e4m3").reshape(F, N, N).swapaxes(1, 2)
    Tq = unpack4(t_words, t_scales).reshape(F, N, D)
    Oq = mxq(f64(o_train), 1, "e4m3")
    rt = f64(a)[:, :, None] * (f64(t_own) - (H @ Tq))
    ro = f64(b)[:, :, None] * (f64(o_own) - (H @ Oq))
    A = mxq(rt.reshape(F * N, D), 0, "e4m3")
    B = mxq(ro.reshape(F * N, P), 0, "e4m3")
    y = f64(gain)[:, None] * (f64(earlier) + (A.T @ B))
    Y = y.reshape(D, P)
    words, scales = planes(Y)
    return y, words, scales

@@ -1,0 +1,413 @@
+from contextlib import ExitStack
+
+import concourse.mybir as mybir
+
+F32 = mybir.dt.float32
+BF16 = mybir.dt.bfloat16
+I32 = mybir.dt.int32
+U32 = mybir.dt.uint32
+U8 = mybir.dt.uint8
+FP8X4 = mybir.dt.float8_e4m3fn_x4
+FP4X4 = mybir.dt.float4_e2m1fn_x4
+ALU = mybir.AluOpType
+ACT = mybir.ActivationFunctionType
+
+FLOPS = 2 * (2 * 1024 * 1024 * 1024 + 2 * 1024 * 1024 * 512 + 2048 * 1024 * 512)
+
+P = 128
+PACK = 4
+W = 512
+
+
+def tile_crossfit_residual_moments_k4_kernel(
+    tc, h_words, h_scales, t_words, t_scales, o_train, t_own, o_own, a, b, earlier, gain, out_0, out_1, out_2
+):
+    nc = tc.nc
+    with ExitStack() as ctx:
+        keep = ctx.enter_context(tc.tile_pool(name="keep", bufs=1))
+        ring = ctx.enter_context(tc.tile_pool(name="ring", bufs=2))
+        psum = ctx.enter_context(tc.psum_pool(name="psum", bufs=1))
+        ctx.enter_context(tc.manual_schedule())
+
+        w_raw = keep.tile([P, 48], BF16, name="w_raw", align_bytes=64)
+
+        def load_weights(c0, c1, src):
+            nc.sync.dma_start(out=w_raw[:, c0:c1].rearrange("p (g j) -> p g j", j=PACK), in_=src)
+
+        hs_raw = keep.tile([P, 4 * 1024], U8, name="hs_raw", align_bytes=64)
+        ts = keep.tile([P, 4 * 1024], U8, name="ts", align_bytes=64)
+        nc.vector.memset(hs_raw[:].bitcast(I32), 0)
+        nc.vector.memset(ts[:].bitcast(I32), 0)
+
+        def load_scales(plane, src):
+            for r in range(4):
+                nc.sync.dma_start(
+                    out=plane[:].bitcast(I32)[r:P:32, :].rearrange("p (g n) -> p g n", g=4),
+                    in_=src[:, r:16:4, :].rearrange("g q n -> q g n").bitcast(I32),
+                )
+
+        raw = {}
+
+        def load_rows(key, rows):
+            tile = keep.tile([P, PACK, W], BF16, name="raw_%s%d%d" % key, align_bytes=64)
+            nc.sync.dma_start(out=tile[:], in_=rows.rearrange("(p j) c -> p j c", j=PACK))
+            raw[key] = tile
+
+        def sample_rows(x, g):
+            return x[g // 2, (g % 2) * W : (g % 2 + 1) * W, :]
+
+        def load_o_train(g):
+            load_rows(("x", g, 0), sample_rows(o_train, g))
+
+        def load_o_own(g):
+            load_rows(("o", g, 0), sample_rows(o_own, g))
+
+        def load_t_own(g, d):
+            load_rows(("t", g, d), sample_rows(t_own, g)[:, d * W : (d + 1) * W])
+
+        def load_earlier(d):
+            load_rows(("y", 0, d), earlier[d * W : (d + 1) * W, :])
+
+        h_raw = {}
+
+        def load_h(g):
+            tile = keep.tile([P, 2, W], U32, name="h_raw%d" % g, align_bytes=64)
+            f, half = divmod(g, 2)
+            src = h_words[2 * f : 2 * f + 2].rearrange("k p n t -> p k (n t)")
+            nc.sync.dma_start(
+                out=tile[:].bitcast(I32), in_=src[:, :, half * 4 * W : (half + 1) * 4 * W].bitcast(I32)
+            )
+            h_raw[g] = tile
+
+        tt = {}
+
+        def load_tt(f, d):
+            tile = keep.tile([P, 2, 2 * W], U8, name="tt%d%d" % (f, d), align_bytes=64)
+            src = t_words[2 * f : 2 * f + 2].rearrange("k p n -> p k n")
+            nc.sync.dma_start(
+                out=tile[:].bitcast(I32), in_=src[:, :, d * 2 * W : (d + 1) * 2 * W].bitcast(I32)
+            )
+            tt[(f, d)] = tile
+
+        load_o_train(0)
+        load_o_train(1)
+        load_h(0)
+        load_scales(hs_raw, h_scales)
+        load_weights(0, 16, b.rearrange("f (h p j) -> p (f h) j", h=2, j=PACK))
+        load_o_own(0)
+        load_h(1)
+        load_o_own(1)
+        load_weights(16, 32, a.rearrange("f (h p j) -> p (f h) j", h=2, j=PACK))
+        load_weights(32, 40, gain.rearrange("(g p j) -> p g j", g=2, j=PACK))
+        load_scales(ts, t_scales)
+        load_tt(0, 0)
+        load_t_own(0, 0)
+        load_t_own(1, 0)
+        load_h(2)
+        load_t_own(2, 0)
+        load_tt(1, 0)
+        load_h(3)
+        load_o_train(2)
+        load_t_own(3, 0)
+        load_o_train(3)
+        load_o_own(2)
+        load_o_own(3)
+        load_tt(0, 1)
+        load_t_own(0, 1)
+        load_t_own(1, 1)
+        load_earlier(0)
+        load_tt(1, 1)
+        load_t_own(2, 1)
+        load_t_own(3, 1)
+        load_earlier(1)
+
+        w_pos = keep.tile([P, 40], F32, name="w_pos")
+        w_neg = keep.tile([P, 32], F32, name="w_neg")
+
+        def widen_weights(c0, c1, c2):
+            nc.vector.tensor_copy(out=w_pos[:, c0:c2], in_=w_raw[:, c0:c2])
+            nc.vector.tensor_scalar(
+                out=w_neg[:, c0:c1], in0=w_raw[:, c0:c1], scalar1=-1.0, scalar2=None, op0=ALU.mult
+            )
+
+        def interleave(engine, dst, src):
+            d4 = dst.rearrange("p (c i j) -> p c j i", i=4, j=PACK)
+            s4 = src.rearrange("p j (c i) -> p c j i", i=4)
+            if engine == "S":
+                nc.scalar.copy(out=d4, in_=s4)
+            else:
+                nc.vector.tensor_copy(out=d4, in_=s4)
+
+        def quantize(codes, scales, src):
+            nc.vector.quantize_mx(out=codes.bitcast(FP8X4), scales=scales, in_=src)
+
+        h_codes, h_sc = {}, {}
+
+        def permute_h_codes(g):
+            tile = keep.tile([P, 2, W], U32, name="h_codes%d" % g, align_bytes=64)
+            nc.vector.tensor_copy(
+                out=tile[:].bitcast(I32).rearrange("p k (t m) -> p k m t", t=PACK),
+                in_=h_raw[g][:].bitcast(I32).rearrange("p k (m t) -> p k m t", t=PACK),
+            )
+            h_codes[g] = tile
+
+        def permute_h_scales(g):
+            tile = keep.tile([P, 2, W], U8, name="h_sc%d" % g, align_bytes=64)
+            f, half = divmod(g, 2)
+            src = hs_raw[:].rearrange("p (g n) -> p g n", g=4)[:, 2 * f : 2 * f + 2, half * W : (half + 1) * W]
+            nc.vector.tensor_copy(
+                out=tile[:].rearrange("p k (t m) -> p k t m", t=PACK),
+                in_=src.rearrange("p k (m t) -> p k t m", t=PACK),
+            )
+            h_sc[g] = tile
+
+        grouped, q_codes, q_scales = {}, {}, {}
+
+        def group_rows(key, engine, src):
+            tile = ring.tile([P, PACK * W], BF16, name="grp_%s%d%d" % key, tag="grp", bufs=3, align_bytes=64)
+            interleave(engine, tile[:], src)
+            grouped[key] = tile
+
+        def quantize_unit(key):
+            codes = keep.tile([P, W], U32, name="qc_%s%d%d" % key, align_bytes=64)
+            scales = keep.tile([P, W], U8, name="qs_%s%d%d" % key, align_bytes=64)
+            quantize(codes[:], scales[:], grouped[key][:])
+            q_codes[key], q_scales[key] = codes, scales
+
+        def weight_col(key, j):
+            kind, g, d = key
+            return {"o": 4 * g, "t": 16 + 4 * g, "y": 32 + 4 * d}[kind] + j
+
+        def by_slot(key, ap):
+            if key[0] == "t":
+                return ap.rearrange("p (m t) -> p t m", t=PACK)
+            return ap.rearrange("p (t m) -> p t m", t=PACK)
+
+        scaled = {}
+
+        def prescale(key, j, engine):
+            tile = ring.tile([P, W], F32, name="sc_%s%d%d_%d" % (key + (j,)), tag="scaled", bufs=10)
+            col = weight_col(key, j)
+            dst = tile[:].rearrange("p (t m) -> p t m", t=PACK)
+            src = by_slot(key, raw[key][:, j, :])
+            if engine == "S":
+                nc.scalar.activation(out=dst, in_=src, func=ACT.Copy, scale=w_pos[:, col : col + 1])
+            elif engine == "V":
+                nc.vector.tensor_scalar(
+                    out=dst, in0=src, scalar1=w_pos[:, col : col + 1], scalar2=None, op0=ALU.mult
+                )
+            else:
+                nc.gpsimd.tensor_scalar(
+                    out=dst, in0=src, scalar1=w_pos[:, col : col + 1], scalar2=0.0, op0=ALU.mult, op1=ALU.add
+                )
+            scaled[(key, j)] = tile
+
+        pred = {}
+
+        def predict(key, j):
+            kind, g, d = key
+            f = g // 2
+            bank = psum.tile([P, W], F32, name="pred_%s%d%d_%d" % (key + (j,)), tag="pred%d" % j)
+            for k in range(2):
+                if kind == "t":
+                    rhs = tt[(f, d)][:, k, :].bitcast(FP4X4)
+                    c0 = (2 * f + k) * 1024 + d * W
+                    rhs_scale = ts[:, c0 : c0 + W]
+                else:
+                    rhs = q_codes[("x", 2 * f + k, 0)][:].bitcast(FP8X4)
+                    rhs_scale = q_scales[("x", 2 * f + k, 0)][:]
+                nc.tensor.matmul_mx(
+                    out=bank[:],
+                    lhsT=h_codes[g][:, k, j * P : (j + 1) * P].bitcast(FP8X4),
+                    lhsT_scale=h_sc[g][:, k, j * P : (j + 1) * P],
+                    rhs=rhs,
+                    rhs_scale=rhs_scale,
+                    start=(k == 0),
+                    stop=(k == 1),
+                )
+            pred[(key, j)] = bank
+
+        resid = {}
+
+        def residual(key, j):
+            if j == 0:
+                resid[key] = ring.tile(
+                    [P, PACK * W], BF16, name="res_%s%d%d" % key, tag="resid", bufs=2, align_bytes=64
+                )
+            col = weight_col(key, j)
+            nc.vector.scalar_tensor_tensor(
+                out=resid[key][:, j * W : (j + 1) * W].rearrange("p (t m) -> p t m", t=PACK),
+                in0=by_slot(key, pred[(key, j)][:]),
+                scalar=w_neg[:, col : col + 1],
+                in1=scaled[(key, j)][:].rearrange("p (t m) -> p t m", t=PACK),
+                op0=ALU.mult,
+                op1=ALU.add,
+            )
+
+        moment = {}
+
+        def moment_pass(d, g, t, lhsT, lhsT_scale):
+            if g == 0:
+                moment[(d, t)] = psum.tile([P, W], F32, name="mom%d_%d" % (d, t), tag="mom%d" % t)
+            nc.tensor.matmul_mx(
+                out=moment[(d, t)][:],
+                lhsT=lhsT.bitcast(FP8X4),
+                lhsT_scale=lhsT_scale,
+                rhs=q_codes[("o", g, 0)][:].bitcast(FP8X4),
+                rhs_scale=q_scales[("o", g, 0)][:],
+                start=(g == 0),
+                stop=(g == 3),
+            )
+
+        def moment_slot(d, g, t):
+            key = ("t", g, d)
+            moment_pass(d, g, t, q_codes[key][:, t * P : (t + 1) * P], q_scales[key][:, t * P : (t + 1) * P])
+
+        def finish(d, t, dst, c0, c1):
+            key = ("y", 0, d)
+            col = weight_col(key, t)
+            nc.vector.scalar_tensor_tensor(
+                out=dst,
+                in0=moment[(d, t)][:, c0:c1],
+                scalar=w_pos[:, col : col + 1],
+                in1=scaled[(key, t)][:, c0:c1],
+                op0=ALU.mult,
+                op1=ALU.add,
+            )
+
+        y_scales = keep.tile([P, 2 * W], U8, name="y_scales", align_bytes=64)
+
+        def store_y(d, tile, c0, c1):
+            nc.sync.dma_start(
+                out=out_0[d * W : (d + 1) * W, :].rearrange("(p t) c -> p t c", t=PACK)[:, :, c0:c1],
+                in_=tile[:].rearrange("p (t c) -> p t c", t=PACK),
+            )
+
+        def quantize_y(d, src, c0, c1):
+            codes = keep.tile([P, c1 - c0], U32, name="y_codes%d_%d" % (d, c0), align_bytes=64)
+            quantize(codes[:], y_scales[:, d * W + c0 : d * W + c1], src)
+            nc.sync.dma_start(
+                out=out_1[d].rearrange("p m t -> p (m t)").bitcast(I32)[:, c0:c1], in_=codes[:].bitcast(I32)
+            )
+
+        x0, x1, x2, x3 = [("x", g, 0) for g in range(4)]
+        units = (
+            [("o", 0, 0), ("o", 1, 0)]
+            + [("t", g, 0) for g in range(4)]
+            + [("o", 2, 0), ("o", 3, 0), ("t", 0, 1), ("t", 1, 1), ("y", 0, 0), ("t", 2, 1), ("t", 3, 1), ("y", 0, 1)]
+        )
+        group_rows(x0, "S", raw[x0][:])
+        group_rows(x1, "V", raw[x1][:])
+        permute_h_codes(0)
+        widen_weights(0, 16, 16)
+        quantize_unit(x0)
+        permute_h_scales(0)
+        quantize_unit(x1)
+        for j in range(PACK):
+            prescale(units[0], j, "S")
+            predict(units[0], j)
+
+        engines = ["SSSS","VVSS","VSSS","VVVV","VVVV","VVSS","VVSS","VVSS","VVSS","VVSS","VVSS","VVSS","VVSS"]
+        y0 = keep.tile([P, PACK * W], F32, name="y0")
+        last = len(units) - 2
+        for s in range(last + 1):
+            key, nxt = units[s], units[s + 1]
+            prev = units[s - 1] if s > 0 else None
+            ahead = None
+            if key[0] != "y":
+                ahead = nxt if nxt[0] != "y" else (units[s + 2] if s + 2 < len(units) else None)
+
+            def drain(j):
+                if key[0] == "y":
+                    finish(0, j, y0[:, j * W : (j + 1) * W], 0, W)
+                    moment_slot(1, 0, j)
+                else:
+                    residual(key, j)
+
+            def close_prev():
+                if prev is None:
+                    return
+                if prev[0] == "y":
+                    quantize_y(0, grouped[prev][:], 0, W)
+                    return
+                quantize_unit(prev)
+                kind, g, d = prev
+                if (kind == "t" and (g < 2 or d == 1) and (d, g) != (1, 0)) or (kind == "o" and g >= 2):
+                    for t in range(PACK):
+                        moment_slot(d, g, t)
+
+            if prev is not None:
+                src = y0 if prev[0] == "y" else resid[prev]
+                group_rows(prev, "S", src[:].rearrange("p (j c) -> p j c", j=PACK))
+            if s in (3, 4):
+                group_rows(("x", s - 1, 0), "S", raw[("x", s - 1, 0)][:])
+            if s == 5:
+                quantize_unit(x3)
+            todo = [(j, engines[s][j]) for j in range(PACK)]
+            for j, e in todo:
+                if e != "V":
+                    prescale(nxt, j, e)
+            on_v = [j for j, e in todo if e == "V"]
+            for j in range(PACK):
+                if j == 3 and s == last:
+                    close_prev()
+                drain(j)
+                if j == 1 and s in (0, 2, 3):
+                    g = {0: 1, 2: 2, 3: 3}[s]
+                    permute_h_codes(g)
+                    permute_h_scales(g)
+                if j < len(on_v):
+                    prescale(nxt, on_v[j], "V")
+                if ahead is not None and j >= 1:
+                    if j == 1:
+                        predict(ahead, 0)
+                    predict(ahead, j)
+            if key[0] == "y":
+                store_y(0, y0, 0, W)
+            if s == 0:
+                widen_weights(16, 32, 40)
+            if s == 4:
+                quantize_unit(x2)
+            if s != last:
+                close_prev()
+
+        key = units[last]
+        res = resid[key][:].rearrange("p (j c) -> p j c", j=PACK)
+        part = {}
+        for t, e in ((0, "V"), (1, "S"), (2, "V"), (3, "S")):
+            part[t] = keep.tile([P, W], BF16, name="part%d" % t, align_bytes=64)
+            interleave(e, part[t][:], res[:, :, t * P : (t + 1) * P])
+        half = W // 2
+        y1 = [keep.tile([P, PACK * half], F32, name="y1_%d" % h) for h in range(2)]
+
+        def close_part(t):
+            codes = keep.tile([P, P], U32, name="part_c%d" % t, align_bytes=64)
+            scales = keep.tile([P, P], U8, name="part_s%d" % t, align_bytes=64)
+            quantize(codes[:], scales[:], part[t][:])
+            moment_pass(1, 3, t, codes[:], scales[:])
+
+        def finish_half(t, h):
+            finish(1, t, y1[h][:, t * half : (t + 1) * half], h * half, (h + 1) * half)
+
+        close_part(0)
+        close_part(2)
+        close_part(1)
+        finish_half(0, 0)
+        close_part(3)
+        for t in (2, 1, 3):
+            finish_half(t, 0)
+        store_y(1, y1[0], 0, half)
+        y_grp = [ring.tile([P, PACK * half], BF16, name="y_grp%d" % h, tag="grp", bufs=3, align_bytes=64) for h in range(2)]
+        interleave("S", y_grp[0][:], y1[0][:].rearrange("p (j c) -> p j c", j=PACK))
+        for t in range(PACK):
+            finish_half(t, 1)
+        store_y(1, y1[1], half, W)
+        quantize_y(1, y_grp[0][:], 0, half)
+        interleave("V", y_grp[1][:], y1[1][:].rearrange("p (j c) -> p j c", j=PACK))
+        quantize_y(1, y_grp[1][:], half, W)
+        for r in range(4):
+            queue = nc.sync if r % 2 == 0 else nc.scalar
+            queue.dma_start(
+                out=out_2[:, r:16:4, :].rearrange("g q n -> q g n").bitcast(I32),
+                in_=y_scales[:].bitcast(I32)[r:P:32, :].rearrange("p (g n) -> p g n", g=2),
+            )

@@ -102,22 +102,22 @@ def tile_crossfit_residual_moments_k4_kernel(
         load_scales(ts, t_scales)
         load_tt(0, 0)
         load_t_own(0, 0)
-        load_t_own(1, 0)
-        load_h(2)
-        load_t_own(2, 0)
-        load_tt(1, 0)
-        load_h(3)
         load_o_train(2)
-        load_t_own(3, 0)
-        load_o_train(3)
-        load_o_own(2)
-        load_o_own(3)
+        load_t_own(1, 0)
         load_tt(0, 1)
         load_t_own(0, 1)
+        load_h(2)
+        load_h(3)
         load_t_own(1, 1)
-        load_earlier(0)
+        load_o_train(3)
+        load_tt(1, 0)
+        load_t_own(2, 0)
+        load_t_own(3, 0)
+        load_o_own(2)
+        load_o_own(3)
         load_tt(1, 1)
         load_t_own(2, 1)
+        load_earlier(0)
         load_t_own(3, 1)
         load_earlier(1)
 
@@ -146,8 +146,8 @@ def tile_crossfit_residual_moments_k4_kernel(
         def permute_h_codes(g):
             tile = keep.tile([P, 2, W], U32, name="h_codes%d" % g, align_bytes=64)
             nc.vector.tensor_copy(
-                out=tile[:].bitcast(I32).rearrange("p k (t m) -> p k m t", t=PACK),
-                in_=h_raw[g][:].bitcast(I32).rearrange("p k (m t) -> p k m t", t=PACK),
+                out=tile[:].bitcast(I32).rearrange("p k (t n m) -> p k n t m", t=PACK, m=4),
+                in_=h_raw[g][:].bitcast(I32).rearrange("p k (n m t) -> p k n t m", t=PACK, m=4),
             )
             h_codes[g] = tile
 
@@ -163,10 +163,13 @@ def tile_crossfit_residual_moments_k4_kernel(
 
         grouped, q_codes, q_scales = {}, {}, {}
 
-        def group_rows(key, engine, src):
-            tile = ring.tile([P, PACK * W], BF16, name="grp_%s%d%d" % key, tag="grp", bufs=3, align_bytes=64)
-            interleave(engine, tile[:], src)
-            grouped[key] = tile
+        def group_rows(key, engine, src, c0=0, c1=W):
+            if c0 == 0:
+                tag, bufs = ("grp_x", 2) if key[0] == "x" else ("grp", 2)
+                grouped[key] = ring.tile(
+                    [P, PACK * W], BF16, name="grp_%s%d%d" % key, tag=tag, bufs=bufs, align_bytes=64
+                )
+            interleave(engine, grouped[key][:, PACK * c0 : PACK * c1], src[:, :, c0:c1])
 
         def quantize_unit(key):
             codes = keep.tile([P, W], U32, name="qc_%s%d%d" % key, align_bytes=64)
@@ -186,7 +189,7 @@ def tile_crossfit_residual_moments_k4_kernel(
         scaled = {}
 
         def prescale(key, j, engine):
-            tile = ring.tile([P, W], F32, name="sc_%s%d%d_%d" % (key + (j,)), tag="scaled", bufs=10)
+            tile = ring.tile([P, W], F32, name="sc_%s%d%d_%d" % (key + (j,)), tag="scaled%d" % j, bufs=(1, 1, 2, 2)[j])
             col = weight_col(key, j)
             dst = tile[:].rearrange("p (t m) -> p t m", t=PACK)
             src = by_slot(key, raw[key][:, j, :])
@@ -291,11 +294,10 @@ def tile_crossfit_residual_moments_k4_kernel(
             )
 
         x0, x1, x2, x3 = [("x", g, 0) for g in range(4)]
-        units = (
-            [("o", 0, 0), ("o", 1, 0)]
-            + [("t", g, 0) for g in range(4)]
-            + [("o", 2, 0), ("o", 3, 0), ("t", 0, 1), ("t", 1, 1), ("y", 0, 0), ("t", 2, 1), ("t", 3, 1), ("y", 0, 1)]
-        )
+        units = [
+            ("o", 0, 0), ("o", 1, 0), ("t", 0, 0), ("t", 1, 0), ("t", 0, 1), ("t", 1, 1),
+            ("t", 2, 0), ("t", 3, 0), ("o", 2, 0), ("o", 3, 0), ("t", 2, 1), ("y", 0, 0), ("t", 3, 1), ("y", 0, 1),
+        ]
         group_rows(x0, "S", raw[x0][:])
         group_rows(x1, "V", raw[x1][:])
         permute_h_codes(0)
@@ -307,7 +309,7 @@ def tile_crossfit_residual_moments_k4_kernel(
             prescale(units[0], j, "S")
             predict(units[0], j)
 
-        engines = ["SSSS","VVSS","VSSS","VVVV","VVVV","VVSS","VVSS","VVSS","VVSS","VVSS","VVSS","VVSS","VVSS"]
+        engines = ["SSSS","GGSG","GGSG","GGSG","GGSS","GGSG","GGSG","GGSS","GGSG","GGSG","GGSG","GGSG","GGSG"]
         y0 = keep.tile([P, PACK * W], F32, name="y0")
         last = len(units) - 2
         for s in range(last + 1):
@@ -316,11 +318,13 @@ def tile_crossfit_residual_moments_k4_kernel(
             ahead = None
             if key[0] != "y":
                 ahead = nxt if nxt[0] != "y" else (units[s + 2] if s + 2 < len(units) else None)
+            early = nxt[0] == "y"
 
             def drain(j):
                 if key[0] == "y":
                     finish(0, j, y0[:, j * W : (j + 1) * W], 0, W)
                     moment_slot(1, 0, j)
+                    moment_slot(1, 1, j)
                 else:
                     residual(key, j)
 
@@ -332,44 +336,44 @@ def tile_crossfit_residual_moments_k4_kernel(
                     return
                 quantize_unit(prev)
                 kind, g, d = prev
-                if (kind == "t" and (g < 2 or d == 1) and (d, g) != (1, 0)) or (kind == "o" and g >= 2):
+                if (kind == "t" and (g < 2) == (d == 0)) or (kind == "o" and g >= 2):
                     for t in range(PACK):
                         moment_slot(d, g, t)
 
             if prev is not None:
                 src = y0 if prev[0] == "y" else resid[prev]
                 group_rows(prev, "S", src[:].rearrange("p (j c) -> p j c", j=PACK))
-            if s in (3, 4):
-                group_rows(("x", s - 1, 0), "S", raw[("x", s - 1, 0)][:])
-            if s == 5:
-                quantize_unit(x3)
-            todo = [(j, engines[s][j]) for j in range(PACK)]
-            for j, e in todo:
-                if e != "V":
-                    prescale(nxt, j, e)
-            on_v = [j for j, e in todo if e == "V"]
+            if s in (2, 3, 5, 6):
+                x = x2 if s < 4 else x3
+                c0 = (W // 2) * (s in (3, 6))
+                group_rows(x, "S", raw[x][:], c0, c0 + W // 2)
+            for j in (3, 2):
+                prescale(nxt, j, engines[s][j])
             for j in range(PACK):
-                if j == 3 and s == last:
+                if j == 3 and early:
                     close_prev()
                 drain(j)
-                if j == 1 and s in (0, 2, 3):
-                    g = {0: 1, 2: 2, 3: 3}[s]
-                    permute_h_codes(g)
-                    permute_h_scales(g)
-                if j < len(on_v):
-                    prescale(nxt, on_v[j], "V")
-                if ahead is not None and j >= 1:
-                    if j == 1:
-                        predict(ahead, 0)
+                if j < 2:
+                    prescale(nxt, j, engines[s][j])
+                if s == 0 and j == 1:
+                    permute_h_codes(1)
+                    permute_h_scales(1)
+                    predict(ahead, 0)
+                if ahead is not None and (s, j) != (0, 0):
                     predict(ahead, j)
             if key[0] == "y":
                 store_y(0, y0, 0, W)
             if s == 0:
                 widen_weights(16, 32, 40)
-            if s == 4:
-                quantize_unit(x2)
-            if s != last:
+            if not early:
                 close_prev()
+            if s == 3:
+                for g in (2, 3):
+                    permute_h_codes(g)
+                    permute_h_scales(g)
+            if s == 6:
+                quantize_unit(x2)
+                quantize_unit(x3)
 
         key = units[last]
         res = resid[key][:].rearrange("p (j c) -> p j c", j=PACK)
@@ -397,7 +401,7 @@ def tile_crossfit_residual_moments_k4_kernel(
         for t in (2, 1, 3):
             finish_half(t, 0)
         store_y(1, y1[0], 0, half)
-        y_grp = [ring.tile([P, PACK * half], BF16, name="y_grp%d" % h, tag="grp", bufs=3, align_bytes=64) for h in range(2)]
+        y_grp = [ring.tile([P, PACK * half], BF16, name="y_grp%d" % h, tag="grp_x", bufs=2, align_bytes=64) for h in range(2)]
         interleave("S", y_grp[0][:], y1[0][:].rearrange("p (j c) -> p j c", j=PACK))
         for t in range(PACK):
             finish_half(t, 1)

@@ -15,8 +15,17 @@ ACT = mybir.ActivationFunctionType
 FLOPS = 2 * (2 * 1024 * 1024 * 1024 + 2 * 1024 * 1024 * 512 + 2048 * 1024 * 512)
 
 P = 128
-PACK = 4
+SLOTS = 4
 W = 512
+HALF = W // 2
+N = 1024
+RUN = 4
+
+UNITS = [
+    ("o", 0, 0), ("o", 1, 0), ("t", 0, 0), ("t", 1, 0), ("t", 0, 1), ("t", 2, 0), ("t", 3, 0),
+    ("o", 2, 0), ("o", 3, 0), ("t", 1, 1), ("t", 2, 1), ("y", 0, 0), ("t", 3, 1), ("y", 0, 1),
+]
+B_COL, A_COL, GAIN_COL, WEIGHT_COLS = 0, 16, 32, 40
 
 
 def tile_crossfit_residual_moments_k4_kernel(
@@ -32,228 +41,206 @@ def tile_crossfit_residual_moments_k4_kernel(
         w_raw = keep.tile([P, 48], BF16, name="w_raw", align_bytes=64)
 
         def load_weights(c0, c1, src):
-            nc.sync.dma_start(out=w_raw[:, c0:c1].rearrange("p (g j) -> p g j", j=PACK), in_=src)
+            nc.sync.dma_start(out=w_raw[:, c0:c1].rearrange("p (g j) -> p g j", j=SLOTS), in_=src)
 
-        hs_raw = keep.tile([P, 4 * 1024], U8, name="hs_raw", align_bytes=64)
-        ts = keep.tile([P, 4 * 1024], U8, name="ts", align_bytes=64)
+        hs_raw = keep.tile([P, N], U8, name="hs_raw", align_bytes=64)
+        hs_packed = keep.tile([P, N], U8, name="hs_packed", align_bytes=64)
+        hs_flat = keep.tile([P, 3 * N], U8, name="hs_flat", align_bytes=64)
+        ts = keep.tile([P, 4 * N], U8, name="ts", align_bytes=64)
         nc.vector.memset(hs_raw[:].bitcast(I32), 0)
         nc.vector.memset(ts[:].bitcast(I32), 0)
+        nc.vector.memset(hs_flat[:].bitcast(I32), 0)
 
-        def load_scales(plane, src):
+        def load_h_scales():
+            for q in range(4):
+                nc.sync.dma_start(
+                    out=hs_raw[:].bitcast(I32)[32 * q : 32 * q + 16, :],
+                    in_=h_scales[:, 4 * q : 4 * q + 4, :].bitcast(I32),
+                )
+
+        def unpack_h_scales(kg):
             for r in range(4):
                 nc.sync.dma_start(
-                    out=plane[:].bitcast(I32)[r:P:32, :].rearrange("p (g n) -> p g n", g=4),
-                    in_=src[:, r:16:4, :].rearrange("g q n -> q g n").bitcast(I32),
+                    out=hs_flat[:, (kg - 1) * N : kg * N].bitcast(I32)[r:P:32, :],
+                    in_=hs_packed[:].bitcast(I32)[4 * kg + r : P : 32, :],
+                )
+
+        def load_t_scales():
+            for r in range(4):
+                nc.sync.dma_start(
+                    out=ts[:].bitcast(I32)[r:P:32, :].rearrange("p (g n) -> p g n", g=4),
+                    in_=t_scales[:, r:16:4, :].rearrange("g q n -> q g n").bitcast(I32),
                 )
 
         raw = {}
 
-        def load_rows(key, rows):
-            tile = keep.tile([P, PACK, W], BF16, name="raw_%s%d%d" % key, align_bytes=64)
-            nc.sync.dma_start(out=tile[:], in_=rows.rearrange("(p j) c -> p j c", j=PACK))
-            raw[key] = tile
-
-        def sample_rows(x, g):
-            return x[g // 2, (g % 2) * W : (g % 2 + 1) * W, :]
-
-        def load_o_train(g):
-            load_rows(("x", g, 0), sample_rows(o_train, g))
-
-        def load_o_own(g):
-            load_rows(("o", g, 0), sample_rows(o_own, g))
-
-        def load_t_own(g, d):
-            load_rows(("t", g, d), sample_rows(t_own, g)[:, d * W : (d + 1) * W])
-
-        def load_earlier(d):
-            load_rows(("y", 0, d), earlier[d * W : (d + 1) * W, :])
+        def load_unit(key):
+            kind, g, d = key
+            if kind == "y":
+                rows = earlier[d * W : (d + 1) * W, :]
+            else:
+                src = {"x": o_train, "o": o_own, "t": t_own}[kind]
+                rows = src[g // 2, (g % 2) * W : (g % 2 + 1) * W, d * W : (d + 1) * W]
+            raw[key] = keep.tile([P, SLOTS, W], BF16, name="raw_%s%d%d" % key, align_bytes=64)
+            nc.sync.dma_start(out=raw[key][:], in_=rows.rearrange("(p j) c -> p j c", j=SLOTS))
 
         h_raw = {}
 
-        def load_h(g):
-            tile = keep.tile([P, 2, W], U32, name="h_raw%d" % g, align_bytes=64)
-            f, half = divmod(g, 2)
-            src = h_words[2 * f : 2 * f + 2].rearrange("k p n t -> p k (n t)")
+        def load_h(g, k0=0, k1=2):
+            if k0 == 0:
+                h_raw[g] = keep.tile([P, 2, W], U32, name="h_raw%d" % g, align_bytes=64)
+            f, side = divmod(g, 2)
+            src = h_words[2 * f + k0 : 2 * f + k1].rearrange("k p n t -> p k (n t)")
             nc.sync.dma_start(
-                out=tile[:].bitcast(I32), in_=src[:, :, half * 4 * W : (half + 1) * 4 * W].bitcast(I32)
+                out=h_raw[g][:, k0:k1, :].bitcast(I32),
+                in_=src[:, :, side * 4 * W : (side + 1) * 4 * W].bitcast(I32),
             )
-            h_raw[g] = tile
 
         tt = {}
 
         def load_tt(f, d):
-            tile = keep.tile([P, 2, 2 * W], U8, name="tt%d%d" % (f, d), align_bytes=64)
+            tt[(f, d)] = keep.tile([P, 2, 2 * W], U8, name="tt%d%d" % (f, d), align_bytes=64)
             src = t_words[2 * f : 2 * f + 2].rearrange("k p n -> p k n")
             nc.sync.dma_start(
-                out=tile[:].bitcast(I32), in_=src[:, :, d * 2 * W : (d + 1) * 2 * W].bitcast(I32)
+                out=tt[(f, d)][:].bitcast(I32), in_=src[:, :, d * 2 * W : (d + 1) * 2 * W].bitcast(I32)
             )
-            tt[(f, d)] = tile
 
-        load_o_train(0)
-        load_o_train(1)
-        load_h(0)
-        load_scales(hs_raw, h_scales)
-        load_weights(0, 16, b.rearrange("f (h p j) -> p (f h) j", h=2, j=PACK))
-        load_o_own(0)
-        load_h(1)
-        load_o_own(1)
-        load_weights(16, 32, a.rearrange("f (h p j) -> p (f h) j", h=2, j=PACK))
-        load_weights(32, 40, gain.rearrange("(g p j) -> p g j", g=2, j=PACK))
-        load_scales(ts, t_scales)
-        load_tt(0, 0)
-        load_t_own(0, 0)
-        load_o_train(2)
-        load_t_own(1, 0)
-        load_tt(0, 1)
-        load_t_own(0, 1)
-        load_h(2)
-        load_h(3)
-        load_t_own(1, 1)
-        load_o_train(3)
-        load_tt(1, 0)
-        load_t_own(2, 0)
-        load_t_own(3, 0)
-        load_o_own(2)
-        load_o_own(3)
-        load_tt(1, 1)
-        load_t_own(2, 1)
-        load_earlier(0)
-        load_t_own(3, 1)
-        load_earlier(1)
+        w_pos = keep.tile([P, WEIGHT_COLS], F32, name="w_pos")
+        w_neg = keep.tile([P, GAIN_COL], F32, name="w_neg")
 
-        w_pos = keep.tile([P, 40], F32, name="w_pos")
-        w_neg = keep.tile([P, 32], F32, name="w_neg")
-
-        def widen_weights(c0, c1, c2):
-            nc.vector.tensor_copy(out=w_pos[:, c0:c2], in_=w_raw[:, c0:c2])
+        def widen_weights(c0, neg_end, pos_end):
+            nc.vector.tensor_copy(out=w_pos[:, c0:pos_end], in_=w_raw[:, c0:pos_end])
             nc.vector.tensor_scalar(
-                out=w_neg[:, c0:c1], in0=w_raw[:, c0:c1], scalar1=-1.0, scalar2=None, op0=ALU.mult
+                out=w_neg[:, c0:neg_end], in0=w_raw[:, c0:neg_end], scalar1=-1.0, scalar2=None, op0=ALU.mult
             )
 
-        def interleave(engine, dst, src):
-            d4 = dst.rearrange("p (c i j) -> p c j i", i=4, j=PACK)
-            s4 = src.rearrange("p j (c i) -> p c j i", i=4)
-            if engine == "S":
-                nc.scalar.copy(out=d4, in_=s4)
-            else:
-                nc.vector.tensor_copy(out=d4, in_=s4)
+        def weight_col(key, j):
+            kind, g, d = key
+            return {"o": B_COL + SLOTS * g, "t": A_COL + SLOTS * g, "y": GAIN_COL + SLOTS * d}[kind] + j
+
+        def interleave(copy, dst, src):
+            copy(
+                out=dst.rearrange("p (c i j) -> p c j i", i=RUN, j=SLOTS),
+                in_=src.rearrange("p j (c i) -> p c j i", i=RUN),
+            )
+
+        def slot_major(ap):
+            return ap.rearrange("p (j c) -> p j c", j=SLOTS)
 
         def quantize(codes, scales, src):
             nc.vector.quantize_mx(out=codes.bitcast(FP8X4), scales=scales, in_=src)
 
-        h_codes, h_sc = {}, {}
+        h_codes = {}
 
-        def permute_h_codes(g):
-            tile = keep.tile([P, 2, W], U32, name="h_codes%d" % g, align_bytes=64)
+        def deal_h_codes(g, k0=0, k1=2):
+            if k0 == 0:
+                h_codes[g] = keep.tile([P, 2, W], U32, name="h_codes%d" % g, align_bytes=64)
             nc.vector.tensor_copy(
-                out=tile[:].bitcast(I32).rearrange("p k (t n m) -> p k n t m", t=PACK, m=4),
-                in_=h_raw[g][:].bitcast(I32).rearrange("p k (n m t) -> p k n t m", t=PACK, m=4),
+                out=h_codes[g][:, k0:k1, :].bitcast(I32).rearrange("p k (j n m) -> p k n j m", j=SLOTS, m=RUN),
+                in_=h_raw[g][:, k0:k1, :].bitcast(I32).rearrange("p k (n m j) -> p k n j m", j=SLOTS, m=RUN),
             )
-            h_codes[g] = tile
 
-        def permute_h_scales(g):
-            tile = keep.tile([P, 2, W], U8, name="h_sc%d" % g, align_bytes=64)
-            f, half = divmod(g, 2)
-            src = hs_raw[:].rearrange("p (g n) -> p g n", g=4)[:, 2 * f : 2 * f + 2, half * W : (half + 1) * W]
+        def deal_h_scales():
             nc.vector.tensor_copy(
-                out=tile[:].rearrange("p k (t m) -> p k t m", t=PACK),
-                in_=src.rearrange("p k (m t) -> p k t m", t=PACK),
+                out=hs_packed[:].rearrange("p (side j m) -> p side j m", side=2, j=SLOTS),
+                in_=hs_raw[:].rearrange("p (side m j) -> p side j m", side=2, j=SLOTS),
             )
-            h_sc[g] = tile
+
+        def h_scale_plane(kind, g, k, j):
+            kg = 2 * (g // 2) + k
+            c0 = (g % 2) * W + j * P
+            if kind == "o" or kg == 0:
+                return hs_packed[4 * kg : P, c0 : c0 + P]
+            return hs_flat[:, (kg - 1) * N + c0 : (kg - 1) * N + c0 + P]
 
         grouped, q_codes, q_scales = {}, {}, {}
 
-        def group_rows(key, engine, src, c0=0, c1=W):
+        def group(key, copy, src, c0=0, c1=W):
             if c0 == 0:
-                tag, bufs = ("grp_x", 2) if key[0] == "x" else ("grp", 2)
+                tag, bufs = ("grp_x", 2) if key[0] == "x" else ("grp", 3)
                 grouped[key] = ring.tile(
-                    [P, PACK * W], BF16, name="grp_%s%d%d" % key, tag=tag, bufs=bufs, align_bytes=64
+                    [P, SLOTS * W], BF16, name="grp_%s%d%d" % key, tag=tag, bufs=bufs, align_bytes=64
                 )
-            interleave(engine, grouped[key][:, PACK * c0 : PACK * c1], src[:, :, c0:c1])
+            interleave(copy, grouped[key][:, SLOTS * c0 : SLOTS * c1], src[:, :, c0:c1])
 
         def quantize_unit(key):
-            codes = keep.tile([P, W], U32, name="qc_%s%d%d" % key, align_bytes=64)
-            scales = keep.tile([P, W], U8, name="qs_%s%d%d" % key, align_bytes=64)
-            quantize(codes[:], scales[:], grouped[key][:])
-            q_codes[key], q_scales[key] = codes, scales
+            q_codes[key] = keep.tile([P, W], U32, name="qc_%s%d%d" % key, align_bytes=64)
+            q_scales[key] = keep.tile([P, W], U8, name="qs_%s%d%d" % key, align_bytes=64)
+            quantize(q_codes[key][:], q_scales[key][:], grouped[key][:])
 
-        def weight_col(key, j):
-            kind, g, d = key
-            return {"o": 4 * g, "t": 16 + 4 * g, "y": 32 + 4 * d}[kind] + j
-
-        def by_slot(key, ap):
+        def in_unit_order(key, ap):
             if key[0] == "t":
-                return ap.rearrange("p (m t) -> p t m", t=PACK)
-            return ap.rearrange("p (t m) -> p t m", t=PACK)
+                return ap.rearrange("p (m t) -> p t m", t=SLOTS)
+            return ap.rearrange("p (t m) -> p t m", t=SLOTS)
 
         scaled = {}
 
-        def prescale(key, j, engine):
-            tile = ring.tile([P, W], F32, name="sc_%s%d%d_%d" % (key + (j,)), tag="scaled%d" % j, bufs=(1, 1, 2, 2)[j])
-            col = weight_col(key, j)
-            dst = tile[:].rearrange("p (t m) -> p t m", t=PACK)
-            src = by_slot(key, raw[key][:, j, :])
-            if engine == "S":
-                nc.scalar.activation(out=dst, in_=src, func=ACT.Copy, scale=w_pos[:, col : col + 1])
-            elif engine == "V":
-                nc.vector.tensor_scalar(
-                    out=dst, in0=src, scalar1=w_pos[:, col : col + 1], scalar2=None, op0=ALU.mult
-                )
+        def prescale(key, j, on_gpsimd):
+            if key == UNITS[-1] and j < 2:
+                tile = keep.tile([P, W], F32, name="sc_last%d" % j, tag="h_raw%d" % j, align_bytes=64)
             else:
+                tag, bufs = ("scaled%d" % ((UNITS.index(key) + j) % 2), 1) if j < 2 else ("scaled%d" % j, 2)
+                tile = ring.tile([P, W], F32, name="sc_%s%d%d_%d" % (key + (j,)), tag=tag, bufs=bufs)
+            col = weight_col(key, j)
+            dst = tile[:].rearrange("p (t m) -> p t m", t=SLOTS)
+            src = in_unit_order(key, raw[key][:, j, :])
+            if on_gpsimd:
                 nc.gpsimd.tensor_scalar(
                     out=dst, in0=src, scalar1=w_pos[:, col : col + 1], scalar2=0.0, op0=ALU.mult, op1=ALU.add
                 )
+            else:
+                nc.scalar.activation(out=dst, in_=src, func=ACT.Copy, scale=w_pos[:, col : col + 1])
             scaled[(key, j)] = tile
 
         pred = {}
 
-        def predict(key, j):
+        def predict(key, j, passes=(0, 1)):
             kind, g, d = key
             f = g // 2
-            bank = psum.tile([P, W], F32, name="pred_%s%d%d_%d" % (key + (j,)), tag="pred%d" % j)
-            for k in range(2):
+            if passes[0] == 0:
+                pred[(key, j)] = psum.tile([P, W], F32, name="pred_%s%d%d_%d" % (key + (j,)), tag="pred%d" % j)
+            for k in passes:
                 if kind == "t":
-                    rhs = tt[(f, d)][:, k, :].bitcast(FP4X4)
-                    c0 = (2 * f + k) * 1024 + d * W
-                    rhs_scale = ts[:, c0 : c0 + W]
+                    c0 = (2 * f + k) * N + d * W
+                    rhs, rhs_scale = tt[(f, d)][:, k, :].bitcast(FP4X4), ts[:, c0 : c0 + W]
                 else:
-                    rhs = q_codes[("x", 2 * f + k, 0)][:].bitcast(FP8X4)
-                    rhs_scale = q_scales[("x", 2 * f + k, 0)][:]
+                    x = ("x", 2 * f + k, 0)
+                    rhs, rhs_scale = q_codes[x][:].bitcast(FP8X4), q_scales[x][:]
                 nc.tensor.matmul_mx(
-                    out=bank[:],
+                    out=pred[(key, j)][:],
                     lhsT=h_codes[g][:, k, j * P : (j + 1) * P].bitcast(FP8X4),
-                    lhsT_scale=h_sc[g][:, k, j * P : (j + 1) * P],
+                    lhsT_scale=h_scale_plane(kind, g, k, j),
                     rhs=rhs,
                     rhs_scale=rhs_scale,
                     start=(k == 0),
                     stop=(k == 1),
                 )
-            pred[(key, j)] = bank
 
         resid = {}
 
-        def residual(key, j):
+        def residual(key, j, t0=0, t1=SLOTS):
+            width = (t1 - t0) * P
             if j == 0:
-                resid[key] = ring.tile(
-                    [P, PACK * W], BF16, name="res_%s%d%d" % key, tag="resid", bufs=2, align_bytes=64
+                resid[(key, t0)] = ring.tile(
+                    [P, SLOTS * width], BF16, name="res_%s%d%d_%d" % (key + (t0,)), tag="resid", bufs=3, align_bytes=64
                 )
             col = weight_col(key, j)
             nc.vector.scalar_tensor_tensor(
-                out=resid[key][:, j * W : (j + 1) * W].rearrange("p (t m) -> p t m", t=PACK),
-                in0=by_slot(key, pred[(key, j)][:]),
+                out=resid[(key, t0)][:, j * width : (j + 1) * width].rearrange("p (t m) -> p t m", m=P),
+                in0=in_unit_order(key, pred[(key, j)][:])[:, t0:t1, :],
                 scalar=w_neg[:, col : col + 1],
-                in1=scaled[(key, j)][:].rearrange("p (t m) -> p t m", t=PACK),
+                in1=scaled[(key, j)][:].rearrange("p (t m) -> p t m", t=SLOTS)[:, t0:t1, :],
                 op0=ALU.mult,
                 op1=ALU.add,
             )
 
-        moment = {}
+        moment_bank = {}
 
         def moment_pass(d, g, t, lhsT, lhsT_scale):
             if g == 0:
-                moment[(d, t)] = psum.tile([P, W], F32, name="mom%d_%d" % (d, t), tag="mom%d" % t)
+                moment_bank[(d, t)] = psum.tile([P, W], F32, name="mom%d_%d" % (d, t), tag="mom%d" % t)
             nc.tensor.matmul_mx(
-                out=moment[(d, t)][:],
+                out=moment_bank[(d, t)][:],
                 lhsT=lhsT.bitcast(FP8X4),
                 lhsT_scale=lhsT_scale,
                 rhs=q_codes[("o", g, 0)][:].bitcast(FP8X4),
@@ -262,153 +249,212 @@ def tile_crossfit_residual_moments_k4_kernel(
                 stop=(g == 3),
             )
 
-        def moment_slot(d, g, t):
+        def moment(d, g, slots):
             key = ("t", g, d)
-            moment_pass(d, g, t, q_codes[key][:, t * P : (t + 1) * P], q_scales[key][:, t * P : (t + 1) * P])
+            for t in slots:
+                moment_pass(d, g, t, q_codes[key][:, t * P : (t + 1) * P], q_scales[key][:, t * P : (t + 1) * P])
 
         def finish(d, t, dst, c0, c1):
             key = ("y", 0, d)
             col = weight_col(key, t)
             nc.vector.scalar_tensor_tensor(
                 out=dst,
-                in0=moment[(d, t)][:, c0:c1],
+                in0=moment_bank[(d, t)][:, c0:c1],
                 scalar=w_pos[:, col : col + 1],
                 in1=scaled[(key, t)][:, c0:c1],
                 op0=ALU.mult,
                 op1=ALU.add,
             )
 
-        y_scales = keep.tile([P, 2 * W], U8, name="y_scales", align_bytes=64)
-
-        def store_y(d, tile, c0, c1):
+        def store_y(d, tile, c0, c1, t0=0, t1=SLOTS):
             nc.sync.dma_start(
-                out=out_0[d * W : (d + 1) * W, :].rearrange("(p t) c -> p t c", t=PACK)[:, :, c0:c1],
-                in_=tile[:].rearrange("p (t c) -> p t c", t=PACK),
+                out=out_0[d * W : (d + 1) * W, :].rearrange("(p t) c -> p t c", t=SLOTS)[:, t0:t1, c0:c1],
+                in_=tile[:, t0 * (c1 - c0) : t1 * (c1 - c0)].rearrange("p (t c) -> p t c", c=c1 - c0),
             )
 
-        def quantize_y(d, src, c0, c1):
-            codes = keep.tile([P, c1 - c0], U32, name="y_codes%d_%d" % (d, c0), align_bytes=64)
+        y_scales = keep.tile([P, 2 * W], U8, name="y_scales", align_bytes=64)
+
+        def quantize_y(d, h, src):
+            c0, c1 = h * HALF, (h + 1) * HALF
+            codes = keep.tile([P, HALF], U32, name="y_codes%d_%d" % (d, h), align_bytes=64)
             quantize(codes[:], y_scales[:, d * W + c0 : d * W + c1], src)
             nc.sync.dma_start(
                 out=out_1[d].rearrange("p m t -> p (m t)").bitcast(I32)[:, c0:c1], in_=codes[:].bitcast(I32)
             )
 
         x0, x1, x2, x3 = [("x", g, 0) for g in range(4)]
-        units = [
-            ("o", 0, 0), ("o", 1, 0), ("t", 0, 0), ("t", 1, 0), ("t", 0, 1), ("t", 1, 1),
-            ("t", 2, 0), ("t", 3, 0), ("o", 2, 0), ("o", 3, 0), ("t", 2, 1), ("y", 0, 0), ("t", 3, 1), ("y", 0, 1),
-        ]
-        group_rows(x0, "S", raw[x0][:])
-        group_rows(x1, "V", raw[x1][:])
-        permute_h_codes(0)
-        widen_weights(0, 16, 16)
+        load_unit(x0)
+        load_h_scales()
+        load_h(0, 0, 1)
+        load_unit(x1)
+        load_h(0, 1, 2)
+        load_weights(B_COL, A_COL, b.rearrange("f (side p j) -> p (f side) j", side=2, j=SLOTS))
+        load_unit(UNITS[0])
+        load_h(1)
+        load_unit(UNITS[1])
+        group(x0, nc.scalar.copy, raw[x0][:], 0, HALF)
+        group(x0, nc.vector.tensor_copy, raw[x0][:], HALF, W)
+        deal_h_scales()
+        load_weights(A_COL, GAIN_COL, a.rearrange("f (side p j) -> p (f side) j", side=2, j=SLOTS))
+        load_weights(GAIN_COL, WEIGHT_COLS, gain.rearrange("(g p j) -> p g j", g=2, j=SLOTS))
+        load_t_scales()
+        unpack_h_scales(1)
+        load_tt(0, 0)
+        load_unit(UNITS[2])
+        load_unit(UNITS[3])
+        load_tt(0, 1)
+        load_unit(UNITS[4])
+        load_h(2)
+        load_unit(x2)
+        unpack_h_scales(2)
+        unpack_h_scales(3)
+        load_tt(1, 0)
+        load_unit(UNITS[5])
+        load_h(3)
+        load_unit(x3)
+        for key in UNITS[6:10]:
+            load_unit(key)
+        load_tt(1, 1)
+        for key in UNITS[10:]:
+            load_unit(key)
+
+        deal_h_codes(0, 0, 1)
         quantize_unit(x0)
-        permute_h_scales(0)
+        for j in range(SLOTS):
+            predict(UNITS[0], j, (0,))
+        group(x1, nc.scalar.copy, raw[x1][:], 0, HALF)
+        group(x1, nc.vector.tensor_copy, raw[x1][:], HALF, W)
+        deal_h_codes(0, 1, 2)
+        widen_weights(B_COL, A_COL, A_COL)
         quantize_unit(x1)
-        for j in range(PACK):
-            prescale(units[0], j, "S")
-            predict(units[0], j)
+        for j in range(SLOTS):
+            prescale(UNITS[0], j, False)
+            predict(UNITS[0], j, (1,))
 
-        engines = ["SSSS","GGSG","GGSG","GGSG","GGSS","GGSG","GGSG","GGSS","GGSG","GGSG","GGSG","GGSG","GGSG"]
-        y0 = keep.tile([P, PACK * W], F32, name="y0")
-        last = len(units) - 2
-        for s in range(last + 1):
-            key, nxt = units[s], units[s + 1]
-            prev = units[s - 1] if s > 0 else None
-            ahead = None
-            if key[0] != "y":
-                ahead = nxt if nxt[0] != "y" else (units[s + 2] if s + 2 < len(units) else None)
-            early = nxt[0] == "y"
+        step_y0 = UNITS.index(("y", 0, 0))
+        step_last = len(UNITS) - 2
+        step_h2 = UNITS.index(("t", 2, 0)) - 2
+        step_h3 = UNITS.index(("t", 3, 0)) - 2
+        step_x3 = UNITS.index(("o", 2, 0)) - 2
+        step_x2 = step_x3 - 1
+        step_moments = UNITS.index(("t", 0, 0)) + 3
+        y0 = keep.tile([P, SLOTS * W], F32, name="y0")
 
-            def drain(j):
-                if key[0] == "y":
+        for s in range(step_last):
+            key, nxt = UNITS[s], UNITS[s + 1]
+            ahead = UNITS[s + 2] if nxt[0] == "y" else nxt
+
+            if s > 0:
+                group(UNITS[s - 1], nc.scalar.copy, slot_major(resid[(UNITS[s - 1], 0)][:]))
+            if s == step_x2 - 1:
+                group(x2, nc.scalar.copy, raw[x2][:])
+            if s == step_x3 - 1:
+                group(x3, nc.scalar.copy, raw[x3][:])
+            prescale(nxt, 3, s != step_x3 + 1)
+            prescale(nxt, 2, s == 0)
+
+            for j in range(SLOTS):
+                catch_up = s == step_y0 - 1 and j == 2
+                if catch_up:
+                    quantize_unit(UNITS[s - 2])
+                if s == step_y0:
                     finish(0, j, y0[:, j * W : (j + 1) * W], 0, W)
-                    moment_slot(1, 0, j)
-                    moment_slot(1, 1, j)
                 else:
                     residual(key, j)
-
-            def close_prev():
-                if prev is None:
-                    return
-                if prev[0] == "y":
-                    quantize_y(0, grouped[prev][:], 0, W)
-                    return
-                quantize_unit(prev)
-                kind, g, d = prev
-                if (kind == "t" and (g < 2) == (d == 0)) or (kind == "o" and g >= 2):
-                    for t in range(PACK):
-                        moment_slot(d, g, t)
-
-            if prev is not None:
-                src = y0 if prev[0] == "y" else resid[prev]
-                group_rows(prev, "S", src[:].rearrange("p (j c) -> p j c", j=PACK))
-            if s in (2, 3, 5, 6):
-                x = x2 if s < 4 else x3
-                c0 = (W // 2) * (s in (3, 6))
-                group_rows(x, "S", raw[x][:], c0, c0 + W // 2)
-            for j in (3, 2):
-                prescale(nxt, j, engines[s][j])
-            for j in range(PACK):
-                if j == 3 and early:
-                    close_prev()
-                drain(j)
                 if j < 2:
-                    prescale(nxt, j, engines[s][j])
+                    prescale(nxt, 1 - j, s != 0)
                 if s == 0 and j == 1:
-                    permute_h_codes(1)
-                    permute_h_scales(1)
+                    deal_h_codes(1)
                     predict(ahead, 0)
-                if ahead is not None and (s, j) != (0, 0):
+                if s != step_y0 and (s, j) != (0, 0):
                     predict(ahead, j)
-            if key[0] == "y":
+                if j == 1 and step_moments <= s < step_moments + 4:
+                    g, pair = divmod(s - step_moments, 2)
+                    moment(0, g, (2 * pair, 2 * pair + 1))
+                if catch_up:
+                    moment(0, 3, range(SLOTS))
+                if s == step_y0:
+                    moment(1, 0, (j,))
+                    moment(1, 1, (j,))
+
+            if s == step_y0:
                 store_y(0, y0, 0, W)
             if s == 0:
-                widen_weights(16, 32, 40)
-            if not early:
-                close_prev()
-            if s == 3:
-                for g in (2, 3):
-                    permute_h_codes(g)
-                    permute_h_scales(g)
-            if s == 6:
+                widen_weights(A_COL, GAIN_COL, WEIGHT_COLS)
+            lag = 2 if s < step_y0 - 1 else 1
+            if s >= lag:
+                done = UNITS[s - lag]
+                quantize_unit(done)
+                if done == ("o", 2, 0):
+                    moment(0, 2, range(SLOTS))
+                if done == ("t", 2, 1):
+                    moment(1, 2, range(SLOTS))
+            if s == step_h2:
+                deal_h_codes(2)
+            if s == step_h3:
+                deal_h_codes(3)
+            if s == step_x2:
                 quantize_unit(x2)
+            if s == step_x3:
                 quantize_unit(x3)
 
-        key = units[last]
-        res = resid[key][:].rearrange("p (j c) -> p j c", j=PACK)
+        key, nxt = UNITS[step_last], UNITS[step_last + 1]
         part = {}
-        for t, e in ((0, "V"), (1, "S"), (2, "V"), (3, "S")):
-            part[t] = keep.tile([P, W], BF16, name="part%d" % t, align_bytes=64)
-            interleave(e, part[t][:], res[:, :, t * P : (t + 1) * P])
-        half = W // 2
-        y1 = [keep.tile([P, PACK * half], F32, name="y1_%d" % h) for h in range(2)]
 
-        def close_part(t):
-            codes = keep.tile([P, P], U32, name="part_c%d" % t, align_bytes=64)
-            scales = keep.tile([P, P], U8, name="part_s%d" % t, align_bytes=64)
-            quantize(codes[:], scales[:], part[t][:])
-            moment_pass(1, 3, t, codes[:], scales[:])
+        def group_part(h):
+            part[h] = keep.tile([P, SLOTS * HALF], BF16, name="part%d" % h, align_bytes=64)
+            interleave(nc.scalar.copy, part[h][:], slot_major(resid[(key, 2 * h)][:]))
+
+        def close_part(h):
+            codes = keep.tile([P, HALF], U32, name="part_c%d" % h, align_bytes=64)
+            scales = keep.tile([P, HALF], U8, name="part_s%d" % h, align_bytes=64)
+            quantize(codes[:], scales[:], part[h][:])
+            for t in range(2):
+                moment_pass(1, 3, 2 * h + t, codes[:, t * P : (t + 1) * P], scales[:, t * P : (t + 1) * P])
+
+        y0_grp = [
+            ring.tile([P, SLOTS * HALF], BF16, name="y0_grp%d" % h, tag="grp", bufs=3, align_bytes=64)
+            for h in range(2)
+        ]
+        interleave(nc.scalar.copy, y0_grp[0][:], slot_major(y0[:])[:, :, 0:HALF])
+        prescale(nxt, 0, False)
+        for j in (3, 2, 1):
+            prescale(nxt, j, True)
+        for h in range(2):
+            for j in range(SLOTS):
+                residual(key, j, 2 * h, 2 * h + 2)
+            group_part(h)
+        interleave(nc.scalar.copy, y0_grp[1][:], slot_major(y0[:])[:, :, HALF:W])
+        close_part(0)
+        quantize_y(0, 0, y0_grp[0][:])
+        close_part(1)
+
+        y1 = [keep.tile([P, SLOTS * HALF], F32, name="y1_%d" % h) for h in range(2)]
 
         def finish_half(t, h):
-            finish(1, t, y1[h][:, t * half : (t + 1) * half], h * half, (h + 1) * half)
+            finish(1, t, y1[h][:, t * HALF : (t + 1) * HALF], h * HALF, (h + 1) * HALF)
 
-        close_part(0)
-        close_part(2)
-        close_part(1)
-        finish_half(0, 0)
-        close_part(3)
-        for t in (2, 1, 3):
+        for t in range(2):
+            for h in range(2):
+                finish_half(t, h)
+        for h in range(2):
+            store_y(1, y1[h], h * HALF, (h + 1) * HALF, 0, 2)
+        y1_grp = [
+            ring.tile([P, SLOTS * HALF], BF16, name="y1_grp%d" % h, tag="grp_x", bufs=2, align_bytes=64)
+            for h in range(2)
+        ]
+        for t in (2, 3):
             finish_half(t, 0)
-        store_y(1, y1[0], 0, half)
-        y_grp = [ring.tile([P, PACK * half], BF16, name="y_grp%d" % h, tag="grp_x", bufs=2, align_bytes=64) for h in range(2)]
-        interleave("S", y_grp[0][:], y1[0][:].rearrange("p (j c) -> p j c", j=PACK))
-        for t in range(PACK):
+        store_y(1, y1[0], 0, HALF, 2, 4)
+        interleave(nc.scalar.copy, y1_grp[0][:], slot_major(y1[0][:]))
+        for t in (2, 3):
             finish_half(t, 1)
-        store_y(1, y1[1], half, W)
-        quantize_y(1, y_grp[0][:], 0, half)
-        interleave("V", y_grp[1][:], y1[1][:].rearrange("p (j c) -> p j c", j=PACK))
-        quantize_y(1, y_grp[1][:], half, W)
+        store_y(1, y1[1], HALF, W, 2, 4)
+        quantize_y(0, 1, y0_grp[1][:])
+        interleave(nc.vector.tensor_copy, y1_grp[1][:], slot_major(y1[1][:]))
+        quantize_y(1, 0, y1_grp[0][:])
+        quantize_y(1, 1, y1_grp[1][:])
+
         for r in range(4):
             queue = nc.sync if r % 2 == 0 else nc.scalar
             queue.dma_start(

@@ -19,6 +19,7 @@ SLOTS = 4
 W = 512
 HALF = W // 2
 N = 1024
+SHARE = 192
 RUN = 4
 
 UNITS = [
@@ -109,10 +110,8 @@ def tile_crossfit_residual_moments_k4_kernel(
         w_neg = keep.tile([P, GAIN_COL], F32, name="w_neg")
 
         def widen_weights(c0, neg_end, pos_end):
-            nc.vector.tensor_copy(out=w_pos[:, c0:pos_end], in_=w_raw[:, c0:pos_end])
-            nc.vector.tensor_scalar(
-                out=w_neg[:, c0:neg_end], in0=w_raw[:, c0:neg_end], scalar1=-1.0, scalar2=None, op0=ALU.mult
-            )
+            nc.scalar.copy(out=w_pos[:, c0:pos_end], in_=w_raw[:, c0:pos_end])
+            nc.scalar.activation(out=w_neg[:, c0:neg_end], in_=w_raw[:, c0:neg_end], func=ACT.Copy, scale=-1.0)
 
         def weight_col(key, j):
             kind, g, d = key
@@ -274,9 +273,8 @@ def tile_crossfit_residual_moments_k4_kernel(
 
         y_scales = keep.tile([P, 2 * W], U8, name="y_scales", align_bytes=64)
 
-        def quantize_y(d, h, src):
-            c0, c1 = h * HALF, (h + 1) * HALF
-            codes = keep.tile([P, HALF], U32, name="y_codes%d_%d" % (d, h), align_bytes=64)
+        def quantize_y(d, c0, c1, src):
+            codes = keep.tile([P, c1 - c0], U32, name="y_codes%d_%d" % (d, c0), align_bytes=64)
             quantize(codes[:], y_scales[:, d * W + c0 : d * W + c1], src)
             nc.sync.dma_start(
                 out=out_1[d].rearrange("p m t -> p (m t)").bitcast(I32)[:, c0:c1], in_=codes[:].bitcast(I32)
@@ -291,22 +289,22 @@ def tile_crossfit_residual_moments_k4_kernel(
         load_weights(B_COL, A_COL, b.rearrange("f (side p j) -> p (f side) j", side=2, j=SLOTS))
         load_unit(UNITS[0])
         load_h(1)
+        load_t_scales()
         load_unit(UNITS[1])
+        load_weights(A_COL, GAIN_COL, a.rearrange("f (side p j) -> p (f side) j", side=2, j=SLOTS))
+        load_weights(GAIN_COL, WEIGHT_COLS, gain.rearrange("(g p j) -> p g j", g=2, j=SLOTS))
+        load_unit(UNITS[2])
         group(x0, nc.scalar.copy, raw[x0][:], 0, HALF)
         group(x0, nc.vector.tensor_copy, raw[x0][:], HALF, W)
         deal_h_scales()
-        load_weights(A_COL, GAIN_COL, a.rearrange("f (side p j) -> p (f side) j", side=2, j=SLOTS))
-        load_weights(GAIN_COL, WEIGHT_COLS, gain.rearrange("(g p j) -> p g j", g=2, j=SLOTS))
-        load_t_scales()
         unpack_h_scales(1)
         load_tt(0, 0)
-        load_unit(UNITS[2])
         load_unit(UNITS[3])
         load_tt(0, 1)
         load_unit(UNITS[4])
+        unpack_h_scales(2)
         load_h(2)
         load_unit(x2)
-        unpack_h_scales(2)
         unpack_h_scales(3)
         load_tt(1, 0)
         load_unit(UNITS[5])
@@ -426,34 +424,18 @@ def tile_crossfit_residual_moments_k4_kernel(
             group_part(h)
         interleave(nc.scalar.copy, y0_grp[1][:], slot_major(y0[:])[:, :, HALF:W])
         close_part(0)
-        quantize_y(0, 0, y0_grp[0][:])
+        quantize_y(0, 0, HALF, y0_grp[0][:])
         close_part(1)
 
-        y1 = [keep.tile([P, SLOTS * HALF], F32, name="y1_%d" % h) for h in range(2)]
-
-        def finish_half(t, h):
-            finish(1, t, y1[h][:, t * HALF : (t + 1) * HALF], h * HALF, (h + 1) * HALF)
-
-        for t in range(2):
-            for h in range(2):
-                finish_half(t, h)
-        for h in range(2):
-            store_y(1, y1[h], h * HALF, (h + 1) * HALF, 0, 2)
-        y1_grp = [
-            ring.tile([P, SLOTS * HALF], BF16, name="y1_grp%d" % h, tag="grp_x", bufs=2, align_bytes=64)
-            for h in range(2)
-        ]
-        for t in (2, 3):
-            finish_half(t, 0)
-        store_y(1, y1[0], 0, HALF, 2, 4)
-        interleave(nc.scalar.copy, y1_grp[0][:], slot_major(y1[0][:]))
-        for t in (2, 3):
-            finish_half(t, 1)
-        store_y(1, y1[1], HALF, W, 2, 4)
-        quantize_y(0, 1, y0_grp[1][:])
-        interleave(nc.vector.tensor_copy, y1_grp[1][:], slot_major(y1[1][:]))
-        quantize_y(1, 0, y1_grp[0][:])
-        quantize_y(1, 1, y1_grp[1][:])
+        y1 = keep.tile([P, SLOTS * W], F32, name="y1")
+        for t in range(SLOTS):
+            finish(1, t, y1[:, t * W : (t + 1) * W], 0, W)
+            store_y(1, y1, 0, W, t, t + 1)
+        y1_grp = ring.tile([P, SLOTS * W], BF16, name="y1_grp", tag="grp_x", bufs=2, align_bytes=64)
+        interleave(nc.scalar.copy, y1_grp[:, 0 : SLOTS * SHARE], slot_major(y1[:])[:, :, 0:SHARE])
+        quantize_y(0, HALF, W, y0_grp[1][:])
+        interleave(nc.vector.tensor_copy, y1_grp[:, SLOTS * SHARE : SLOTS * W], slot_major(y1[:])[:, :, SHARE:W])
+        quantize_y(1, 0, W, y1_grp[:])
 
         for r in range(4):
             queue = nc.sync if r % 2 == 0 else nc.scalar

from contextlib import ExitStack

import concourse.mybir as mybir

F32 = mybir.dt.float32
BF16 = mybir.dt.bfloat16
I32 = mybir.dt.int32
U32 = mybir.dt.uint32
U8 = mybir.dt.uint8
FP8X4 = mybir.dt.float8_e4m3fn_x4
FP4X4 = mybir.dt.float4_e2m1fn_x4
ALU = mybir.AluOpType
ACT = mybir.ActivationFunctionType

FLOPS = 2 * (2 * 1024 * 1024 * 1024 + 2 * 1024 * 1024 * 512 + 2048 * 1024 * 512)

P = 128
SLOTS = 4
W = 512
HALF = W // 2
N = 1024
SHARE = 192
RUN = 4

UNITS = [
    ("o", 0, 0), ("o", 1, 0), ("t", 0, 0), ("t", 1, 0), ("t", 0, 1), ("t", 2, 0), ("t", 3, 0),
    ("o", 2, 0), ("o", 3, 0), ("t", 1, 1), ("t", 2, 1), ("y", 0, 0), ("t", 3, 1), ("y", 0, 1),
]
B_COL, A_COL, GAIN_COL, WEIGHT_COLS = 0, 16, 32, 40


def tile_crossfit_residual_moments_k4_kernel(
    tc, h_words, h_scales, t_words, t_scales, o_train, t_own, o_own, a, b, earlier, gain, out_0, out_1, out_2
):
    nc = tc.nc
    with ExitStack() as ctx:
        keep = ctx.enter_context(tc.tile_pool(name="keep", bufs=1))
        ring = ctx.enter_context(tc.tile_pool(name="ring", bufs=2))
        psum = ctx.enter_context(tc.psum_pool(name="psum", bufs=1))
        ctx.enter_context(tc.manual_schedule())

        w_raw = keep.tile([P, 48], BF16, name="w_raw", align_bytes=64)

        def load_weights(c0, c1, src):
            nc.sync.dma_start(out=w_raw[:, c0:c1].rearrange("p (g j) -> p g j", j=SLOTS), in_=src)

        hs_raw = keep.tile([P, N], U8, name="hs_raw", align_bytes=64)
        hs_packed = keep.tile([P, N], U8, name="hs_packed", align_bytes=64)
        hs_flat = keep.tile([P, 3 * N], U8, name="hs_flat", align_bytes=64)
        ts = keep.tile([P, 4 * N], U8, name="ts", align_bytes=64)
        nc.vector.memset(hs_raw[:].bitcast(I32), 0)
        nc.vector.memset(ts[:].bitcast(I32), 0)
        nc.vector.memset(hs_flat[:].bitcast(I32), 0)

        def load_h_scales():
            for q in range(4):
                nc.sync.dma_start(
                    out=hs_raw[:].bitcast(I32)[32 * q : 32 * q + 16, :],
                    in_=h_scales[:, 4 * q : 4 * q + 4, :].bitcast(I32),
                )

        def unpack_h_scales(kg):
            for r in range(4):
                nc.sync.dma_start(
                    out=hs_flat[:, (kg - 1) * N : kg * N].bitcast(I32)[r:P:32, :],
                    in_=hs_packed[:].bitcast(I32)[4 * kg + r : P : 32, :],
                )

        def load_t_scales():
            for r in range(4):
                nc.sync.dma_start(
                    out=ts[:].bitcast(I32)[r:P:32, :].rearrange("p (g n) -> p g n", g=4),
                    in_=t_scales[:, r:16:4, :].rearrange("g q n -> q g n").bitcast(I32),
                )

        raw = {}

        def load_unit(key):
            kind, g, d = key
            if kind == "y":
                rows = earlier[d * W : (d + 1) * W, :]
            else:
                src = {"x": o_train, "o": o_own, "t": t_own}[kind]
                rows = src[g // 2, (g % 2) * W : (g % 2 + 1) * W, d * W : (d + 1) * W]
            raw[key] = keep.tile([P, SLOTS, W], BF16, name="raw_%s%d%d" % key, align_bytes=64)
            nc.sync.dma_start(out=raw[key][:], in_=rows.rearrange("(p j) c -> p j c", j=SLOTS))

        h_raw = {}

        def load_h(g, k0=0, k1=2):
            if k0 == 0:
                h_raw[g] = keep.tile([P, 2, W], U32, name="h_raw%d" % g, align_bytes=64)
            f, side = divmod(g, 2)
            src = h_words[2 * f + k0 : 2 * f + k1].rearrange("k p n t -> p k (n t)")
            nc.sync.dma_start(
                out=h_raw[g][:, k0:k1, :].bitcast(I32),
                in_=src[:, :, side * 4 * W : (side + 1) * 4 * W].bitcast(I32),
            )

        tt = {}

        def load_tt(f, d):
            tt[(f, d)] = keep.tile([P, 2, 2 * W], U8, name="tt%d%d" % (f, d), align_bytes=64)
            src = t_words[2 * f : 2 * f + 2].rearrange("k p n -> p k n")
            nc.sync.dma_start(
                out=tt[(f, d)][:].bitcast(I32), in_=src[:, :, d * 2 * W : (d + 1) * 2 * W].bitcast(I32)
            )

        w_pos = keep.tile([P, WEIGHT_COLS], F32, name="w_pos")
        w_neg = keep.tile([P, GAIN_COL], F32, name="w_neg")

        def widen_weights(c0, neg_end, pos_end):
            nc.scalar.copy(out=w_pos[:, c0:pos_end], in_=w_raw[:, c0:pos_end])
            nc.scalar.activation(out=w_neg[:, c0:neg_end], in_=w_raw[:, c0:neg_end], func=ACT.Copy, scale=-1.0)

        def weight_col(key, j):
            kind, g, d = key
            return {"o": B_COL + SLOTS * g, "t": A_COL + SLOTS * g, "y": GAIN_COL + SLOTS * d}[kind] + j

        def interleave(copy, dst, src):
            copy(
                out=dst.rearrange("p (c i j) -> p c j i", i=RUN, j=SLOTS),
                in_=src.rearrange("p j (c i) -> p c j i", i=RUN),
            )

        def slot_major(ap):
            return ap.rearrange("p (j c) -> p j c", j=SLOTS)

        def quantize(codes, scales, src):
            nc.vector.quantize_mx(out=codes.bitcast(FP8X4), scales=scales, in_=src)

        h_codes = {}

        def deal_h_codes(g, k0=0, k1=2):
            if k0 == 0:
                h_codes[g] = keep.tile([P, 2, W], U32, name="h_codes%d" % g, align_bytes=64)
            nc.vector.tensor_copy(
                out=h_codes[g][:, k0:k1, :].bitcast(I32).rearrange("p k (j n m) -> p k n j m", j=SLOTS, m=RUN),
                in_=h_raw[g][:, k0:k1, :].bitcast(I32).rearrange("p k (n m j) -> p k n j m", j=SLOTS, m=RUN),
            )

        def deal_h_scales():
            nc.vector.tensor_copy(
                out=hs_packed[:].rearrange("p (side j m) -> p side j m", side=2, j=SLOTS),
                in_=hs_raw[:].rearrange("p (side m j) -> p side j m", side=2, j=SLOTS),
            )

        def h_scale_plane(kind, g, k, j):
            kg = 2 * (g // 2) + k
            c0 = (g % 2) * W + j * P
            if kind == "o" or kg == 0:
                return hs_packed[4 * kg : P, c0 : c0 + P]
            return hs_flat[:, (kg - 1) * N + c0 : (kg - 1) * N + c0 + P]

        grouped, q_codes, q_scales = {}, {}, {}

        def group(key, copy, src, c0=0, c1=W):
            if c0 == 0:
                tag, bufs = ("grp_x", 2) if key[0] == "x" else ("grp", 3)
                grouped[key] = ring.tile(
                    [P, SLOTS * W], BF16, name="grp_%s%d%d" % key, tag=tag, bufs=bufs, align_bytes=64
                )
            interleave(copy, grouped[key][:, SLOTS * c0 : SLOTS * c1], src[:, :, c0:c1])

        def quantize_unit(key):
            q_codes[key] = keep.tile([P, W], U32, name="qc_%s%d%d" % key, align_bytes=64)
            q_scales[key] = keep.tile([P, W], U8, name="qs_%s%d%d" % key, align_bytes=64)
            quantize(q_codes[key][:], q_scales[key][:], grouped[key][:])

        def in_unit_order(key, ap):
            if key[0] == "t":
                return ap.rearrange("p (m t) -> p t m", t=SLOTS)
            return ap.rearrange("p (t m) -> p t m", t=SLOTS)

        scaled = {}

        def prescale(key, j, on_gpsimd):
            if key == UNITS[-1] and j < 2:
                tile = keep.tile([P, W], F32, name="sc_last%d" % j, tag="h_raw%d" % j, align_bytes=64)
            else:
                tag, bufs = ("scaled%d" % ((UNITS.index(key) + j) % 2), 1) if j < 2 else ("scaled%d" % j, 2)
                tile = ring.tile([P, W], F32, name="sc_%s%d%d_%d" % (key + (j,)), tag=tag, bufs=bufs)
            col = weight_col(key, j)
            dst = tile[:].rearrange("p (t m) -> p t m", t=SLOTS)
            src = in_unit_order(key, raw[key][:, j, :])
            if on_gpsimd:
                nc.gpsimd.tensor_scalar(
                    out=dst, in0=src, scalar1=w_pos[:, col : col + 1], scalar2=0.0, op0=ALU.mult, op1=ALU.add
                )
            else:
                nc.scalar.activation(out=dst, in_=src, func=ACT.Copy, scale=w_pos[:, col : col + 1])
            scaled[(key, j)] = tile

        pred = {}

        def predict(key, j, passes=(0, 1)):
            kind, g, d = key
            f = g // 2
            if passes[0] == 0:
                pred[(key, j)] = psum.tile([P, W], F32, name="pred_%s%d%d_%d" % (key + (j,)), tag="pred%d" % j)
            for k in passes:
                if kind == "t":
                    c0 = (2 * f + k) * N + d * W
                    rhs, rhs_scale = tt[(f, d)][:, k, :].bitcast(FP4X4), ts[:, c0 : c0 + W]
                else:
                    x = ("x", 2 * f + k, 0)
                    rhs, rhs_scale = q_codes[x][:].bitcast(FP8X4), q_scales[x][:]
                nc.tensor.matmul_mx(
                    out=pred[(key, j)][:],
                    lhsT=h_codes[g][:, k, j * P : (j + 1) * P].bitcast(FP8X4),
                    lhsT_scale=h_scale_plane(kind, g, k, j),
                    rhs=rhs,
                    rhs_scale=rhs_scale,
                    start=(k == 0),
                    stop=(k == 1),
                )

        resid = {}

        def residual(key, j, t0=0, t1=SLOTS):
            width = (t1 - t0) * P
            if j == 0:
                resid[(key, t0)] = ring.tile(
                    [P, SLOTS * width], BF16, name="res_%s%d%d_%d" % (key + (t0,)), tag="resid", bufs=3, align_bytes=64
                )
            col = weight_col(key, j)
            nc.vector.scalar_tensor_tensor(
                out=resid[(key, t0)][:, j * width : (j + 1) * width].rearrange("p (t m) -> p t m", m=P),
                in0=in_unit_order(key, pred[(key, j)][:])[:, t0:t1, :],
                scalar=w_neg[:, col : col + 1],
                in1=scaled[(key, j)][:].rearrange("p (t m) -> p t m", t=SLOTS)[:, t0:t1, :],
                op0=ALU.mult,
                op1=ALU.add,
            )

        moment_bank = {}

        def moment_pass(d, g, t, lhsT, lhsT_scale):
            if g == 0:
                moment_bank[(d, t)] = psum.tile([P, W], F32, name="mom%d_%d" % (d, t), tag="mom%d" % t)
            nc.tensor.matmul_mx(
                out=moment_bank[(d, t)][:],
                lhsT=lhsT.bitcast(FP8X4),
                lhsT_scale=lhsT_scale,
                rhs=q_codes[("o", g, 0)][:].bitcast(FP8X4),
                rhs_scale=q_scales[("o", g, 0)][:],
                start=(g == 0),
                stop=(g == 3),
            )

        def moment(d, g, slots):
            key = ("t", g, d)
            for t in slots:
                moment_pass(d, g, t, q_codes[key][:, t * P : (t + 1) * P], q_scales[key][:, t * P : (t + 1) * P])

        def finish(d, t, dst, c0, c1):
            key = ("y", 0, d)
            col = weight_col(key, t)
            nc.vector.scalar_tensor_tensor(
                out=dst,
                in0=moment_bank[(d, t)][:, c0:c1],
                scalar=w_pos[:, col : col + 1],
                in1=scaled[(key, t)][:, c0:c1],
                op0=ALU.mult,
                op1=ALU.add,
            )

        def store_y(d, tile, c0, c1, t0=0, t1=SLOTS):
            nc.sync.dma_start(
                out=out_0[d * W : (d + 1) * W, :].rearrange("(p t) c -> p t c", t=SLOTS)[:, t0:t1, c0:c1],
                in_=tile[:, t0 * (c1 - c0) : t1 * (c1 - c0)].rearrange("p (t c) -> p t c", c=c1 - c0),
            )

        y_scales = keep.tile([P, 2 * W], U8, name="y_scales", align_bytes=64)

        def quantize_y(d, c0, c1, src):
            codes = keep.tile([P, c1 - c0], U32, name="y_codes%d_%d" % (d, c0), align_bytes=64)
            quantize(codes[:], y_scales[:, d * W + c0 : d * W + c1], src)
            nc.sync.dma_start(
                out=out_1[d].rearrange("p m t -> p (m t)").bitcast(I32)[:, c0:c1], in_=codes[:].bitcast(I32)
            )

        x0, x1, x2, x3 = [("x", g, 0) for g in range(4)]
        load_unit(x0)
        load_h_scales()
        load_h(0, 0, 1)
        load_unit(x1)
        load_h(0, 1, 2)
        load_weights(B_COL, A_COL, b.rearrange("f (side p j) -> p (f side) j", side=2, j=SLOTS))
        load_unit(UNITS[0])
        load_h(1)
        load_t_scales()
        load_unit(UNITS[1])
        load_weights(A_COL, GAIN_COL, a.rearrange("f (side p j) -> p (f side) j", side=2, j=SLOTS))
        load_weights(GAIN_COL, WEIGHT_COLS, gain.rearrange("(g p j) -> p g j", g=2, j=SLOTS))
        load_unit(UNITS[2])
        group(x0, nc.scalar.copy, raw[x0][:], 0, HALF)
        group(x0, nc.vector.tensor_copy, raw[x0][:], HALF, W)
        deal_h_scales()
        unpack_h_scales(1)
        load_tt(0, 0)
        load_unit(UNITS[3])
        load_tt(0, 1)
        load_unit(UNITS[4])
        unpack_h_scales(2)
        load_h(2)
        load_unit(x2)
        unpack_h_scales(3)
        load_tt(1, 0)
        load_unit(UNITS[5])
        load_h(3)
        load_unit(x3)
        for key in UNITS[6:10]:
            load_unit(key)
        load_tt(1, 1)
        for key in UNITS[10:]:
            load_unit(key)

        deal_h_codes(0, 0, 1)
        quantize_unit(x0)
        for j in range(SLOTS):
            predict(UNITS[0], j, (0,))
        group(x1, nc.scalar.copy, raw[x1][:], 0, HALF)
        group(x1, nc.vector.tensor_copy, raw[x1][:], HALF, W)
        deal_h_codes(0, 1, 2)
        widen_weights(B_COL, A_COL, A_COL)
        quantize_unit(x1)
        for j in range(SLOTS):
            prescale(UNITS[0], j, False)
            predict(UNITS[0], j, (1,))

        step_y0 = UNITS.index(("y", 0, 0))
        step_last = len(UNITS) - 2
        step_h2 = UNITS.index(("t", 2, 0)) - 2
        step_h3 = UNITS.index(("t", 3, 0)) - 2
        step_x3 = UNITS.index(("o", 2, 0)) - 2
        step_x2 = step_x3 - 1
        step_moments = UNITS.index(("t", 0, 0)) + 3
        y0 = keep.tile([P, SLOTS * W], F32, name="y0")

        for s in range(step_last):
            key, nxt = UNITS[s], UNITS[s + 1]
            ahead = UNITS[s + 2] if nxt[0] == "y" else nxt

            if s > 0:
                group(UNITS[s - 1], nc.scalar.copy, slot_major(resid[(UNITS[s - 1], 0)][:]))
            if s == step_x2 - 1:
                group(x2, nc.scalar.copy, raw[x2][:])
            if s == step_x3 - 1:
                group(x3, nc.scalar.copy, raw[x3][:])
            prescale(nxt, 3, s != step_x3 + 1)
            prescale(nxt, 2, s == 0)

            for j in range(SLOTS):
                catch_up = s == step_y0 - 1 and j == 2
                if catch_up:
                    quantize_unit(UNITS[s - 2])
                if s == step_y0:
                    finish(0, j, y0[:, j * W : (j + 1) * W], 0, W)
                else:
                    residual(key, j)
                if j < 2:
                    prescale(nxt, 1 - j, s != 0)
                if s == 0 and j == 1:
                    deal_h_codes(1)
                    predict(ahead, 0)
                if s != step_y0 and (s, j) != (0, 0):
                    predict(ahead, j)
                if j == 1 and step_moments <= s < step_moments + 4:
                    g, pair = divmod(s - step_moments, 2)
                    moment(0, g, (2 * pair, 2 * pair + 1))
                if catch_up:
                    moment(0, 3, range(SLOTS))
                if s == step_y0:
                    moment(1, 0, (j,))
                    moment(1, 1, (j,))

            if s == step_y0:
                store_y(0, y0, 0, W)
            if s == 0:
                widen_weights(A_COL, GAIN_COL, WEIGHT_COLS)
            lag = 2 if s < step_y0 - 1 else 1
            if s >= lag:
                done = UNITS[s - lag]
                quantize_unit(done)
                if done == ("o", 2, 0):
                    moment(0, 2, range(SLOTS))
                if done == ("t", 2, 1):
                    moment(1, 2, range(SLOTS))
            if s == step_h2:
                deal_h_codes(2)
            if s == step_h3:
                deal_h_codes(3)
            if s == step_x2:
                quantize_unit(x2)
            if s == step_x3:
                quantize_unit(x3)

        key, nxt = UNITS[step_last], UNITS[step_last + 1]
        part = {}

        def group_part(h):
            part[h] = keep.tile([P, SLOTS * HALF], BF16, name="part%d" % h, align_bytes=64)
            interleave(nc.scalar.copy, part[h][:], slot_major(resid[(key, 2 * h)][:]))

        def close_part(h):
            codes = keep.tile([P, HALF], U32, name="part_c%d" % h, align_bytes=64)
            scales = keep.tile([P, HALF], U8, name="part_s%d" % h, align_bytes=64)
            quantize(codes[:], scales[:], part[h][:])
            for t in range(2):
                moment_pass(1, 3, 2 * h + t, codes[:, t * P : (t + 1) * P], scales[:, t * P : (t + 1) * P])

        y0_grp = [
            ring.tile([P, SLOTS * HALF], BF16, name="y0_grp%d" % h, tag="grp", bufs=3, align_bytes=64)
            for h in range(2)
        ]
        interleave(nc.scalar.copy, y0_grp[0][:], slot_major(y0[:])[:, :, 0:HALF])
        prescale(nxt, 0, False)
        for j in (3, 2, 1):
            prescale(nxt, j, True)
        for h in range(2):
            for j in range(SLOTS):
                residual(key, j, 2 * h, 2 * h + 2)
            group_part(h)
        interleave(nc.scalar.copy, y0_grp[1][:], slot_major(y0[:])[:, :, HALF:W])
        close_part(0)
        quantize_y(0, 0, HALF, y0_grp[0][:])
        close_part(1)

        y1 = keep.tile([P, SLOTS * W], F32, name="y1")
        for t in range(SLOTS):
            finish(1, t, y1[:, t * W : (t + 1) * W], 0, W)
            store_y(1, y1, 0, W, t, t + 1)
        y1_grp = ring.tile([P, SLOTS * W], BF16, name="y1_grp", tag="grp_x", bufs=2, align_bytes=64)
        interleave(nc.scalar.copy, y1_grp[:, 0 : SLOTS * SHARE], slot_major(y1[:])[:, :, 0:SHARE])
        quantize_y(0, HALF, W, y0_grp[1][:])
        interleave(nc.vector.tensor_copy, y1_grp[:, SLOTS * SHARE : SLOTS * W], slot_major(y1[:])[:, :, SHARE:W])
        quantize_y(1, 0, W, y1_grp[:])

        for r in range(4):
            queue = nc.sync if r % 2 == 0 else nc.scalar
            queue.dma_start(
                out=out_2[:, r:16:4, :].rearrange("g q n -> q g n").bitcast(I32),
                in_=y_scales[:].bitcast(I32)[r:P:32, :].rearrange("p (g n) -> p g n", g=2),
            )
